import numpy as np
import ml_dtypes


def mxq(x, axis, fmt="e4m3"):
    dtype, down = {"e4m3": (ml_dtypes.float8_e4m3fn, 7), "e5m2": (ml_dtypes.float8_e5m2, 14)}[fmt]
    v = np.moveaxis(np.asarray(x, np.float32).astype(ml_dtypes.bfloat16).astype(np.float64), axis, -1)
    blocks = v.reshape(v.shape[:-1] + (-1, 32))
    amax = np.abs(blocks).max(-1, keepdims=True)
    byte = np.maximum(np.where(amax > 0, np.frexp(amax)[1] - 1 + 127, 0) - down, 1)
    scale = np.exp2(byte - 127.0)
    codes = (blocks / scale).astype(np.float32).astype(dtype).astype(np.float64)
    return np.moveaxis((codes * scale).reshape(v.shape), -1, axis)


WIDE = False


def mx_kscale(k):
    if not WIDE:
        return np.ones(k)
    levels = np.array([30, -30])
    if k % 512:
        return np.exp2(np.random.permutation(np.resize(levels, k // 32))).repeat(32)
    a = np.empty((k // 512, 16))
    for p in range(k // 512):
        a[p, :8] = np.random.permutation(np.resize(levels, 8))
        for g in range(8):
            far = levels[np.abs(levels - a[p, g]) >= 10]
            a[p, g + 8] = far[np.random.randint(len(far))]
    return np.exp2(a.ravel()).repeat(32)


def f64(x):
    return np.asarray(x).astype(np.float64)


def striped(idx):
    return np.tile(np.asarray(idx).reshape(-1, 16).T, (8, 1)).astype(np.uint16)


def unstriped(offs):
    return offs[:16].T.reshape(-1).astype(np.int64)


E2M1 = np.array([0.0, 0.5, 1.0, 1.5, 2.0, 3.0, 4.0, 6.0, -0.0, -0.5, -1.0, -1.5, -2.0, -3.0, -4.0, -6.0])


def pack_weight(w, fmt):
    k, n = w.shape
    w = f64(np.asarray(w, np.float32).astype(ml_dtypes.bfloat16)).reshape(k // 32, 32, n)
    amax = np.abs(w).max(1)
    if fmt in ("e4m3", "e5m2"):
        byte = np.frexp(amax)[1] - 1 + 127 - (7 if fmt == "e4m3" else 14)
    else:
        mant, ex = np.frexp(amax / 6.0)
        byte = np.where(mant > 0.5, ex, ex - 1) + 127
    byte = np.clip(np.where(amax > 0, byte, 1), 1, 254)
    scaled = (w * np.exp2(127.0 - byte)[:, None, :]).reshape(k, n).astype(np.float32)
    by_word = np.ascontiguousarray(scaled.reshape(k // 512, 128, 4, n).transpose(0, 1, 3, 2))
    if fmt in ("e4m3", "e5m2"):
        words = by_word.astype(ml_dtypes.float8_e4m3fn if fmt == "e4m3" else ml_dtypes.float8_e5m2).view(np.uint8)
    else:
        c = by_word.astype(ml_dtypes.float4_e2m1fn).view(np.uint8) & 0xF
        words = (c[..., 0::2] | (c[..., 1::2] << 4)).reshape(k // 512, 128, 2 * n)
    return np.ascontiguousarray(words), np.ascontiguousarray(byte.astype(np.uint8).reshape(k // 512, 16, n))


def unpack_weight(words, scales, fmt):
    g, _, n = scales.shape
    words = np.ascontiguousarray(words).reshape(g, 128, n, -1)
    if fmt in ("e4m3", "e5m2"):
        vals = words.view(ml_dtypes.float8_e4m3fn if fmt == "e4m3" else ml_dtypes.float8_e5m2).astype(np.float64)
    else:
        nib = np.empty((g, 128, n, 4), np.uint8)
        nib[..., 0::2] = words & 0xF
        nib[..., 1::2] = words >> 4
        vals = E2M1[nib]
    vals = vals * np.repeat(np.exp2(scales.astype(np.float64) - 127.0), 8, axis=1)[..., None]
    return vals.transpose(0, 1, 3, 2).reshape(g * 512, n)


K, T, J, N, M = 1024, 1024, 256, 256, 128


def setup_inputs():
    n = np.random.standard_normal
    idx = np.random.permutation(T)[:J]
    idx2 = np.random.permutation(N)[:M]
    idx3 = np.random.permutation(N)[:M]
    fk = mx_kscale(K)
    xtp = pack_weight(n((K, T)) * np.random.uniform(0.4, 1.6, (1, T)) / fk[:, None], "e2m1")
    wap = pack_weight(n((K, N)) * 1 / np.sqrt(K) * fk[:, None], "e5m2")
    return {
        "xt_words": xtp[0],
        "xt_scales": xtp[1],
        "wa_words": wap[0],
        "wa_scales": wap[1],
        "wb": (n((K, N)) * 1 / np.sqrt(K) * fk[:, None]).astype(np.float32),
        "bi": (np.random.uniform(-0.6, 0.6, (1, N))).astype(np.float32),
        "cj": (np.random.uniform(0.5, 2.0, (J, 1))).astype(np.float32),
        "offs": striped(idx),
        "offs2": striped(idx2),
        "offs3": striped(idx3),
    }


def reference(xt_words, xt_scales, wa_words, wa_scales, wb, bi, cj, offs, offs2, offs3):
    idx = unstriped(offs)
    idx2 = unstriped(offs2)
    idx3 = unstriped(offs3)
    xtu = unpack_weight(xt_words, xt_scales, "e2m1")
    wau = unpack_weight(wa_words, wa_scales, "e5m2")
    xtidxg = xtu[:, idx]
    a = xtidxg.T @ wau
    wbq = mxq(f64(wb), 0, "e5m2")
    b0 = xtidxg.T @ wbq
    b2 = b0 + f64(bi)
    y = (a[:, idx2] - b2[:, idx3]) * f64(cj)
    return y

@@ -1,0 +1,140 @@
+from contextlib import ExitStack
+
+import concourse.mybir as mybir
+from concourse.masks import make_identity
+
+K, T, J, N, M = 1024, 1024, 256, 256, 128
+FLOPS = 2 * 2 * K * J * N
+
+F32 = mybir.dt.float32
+BF16 = mybir.dt.bfloat16
+I32 = mybir.dt.int32
+U32 = mybir.dt.uint32
+U16 = mybir.dt.uint16
+U8 = mybir.dt.uint8
+E5M2X4 = mybir.dt.float8_e5m2_x4
+E2M1X4 = mybir.dt.float4_e2m1fn_x4
+ALU = mybir.AluOpType
+COPY = mybir.ActivationFunctionType.Copy
+
+P = 128
+PACK = 4
+PASSES = K // (P * PACK)
+HALVES = J // P
+VECTOR_COLS = (128, 168)
+
+
+def tile_list_rows_onetoken_lookedtarget_kernel(
+    tc, xt_words, xt_scales, wa_words, wa_scales, wb, bi, cj, offs, offs2, offs3, out
+):
+    nc = tc.nc
+    with ExitStack() as ctx:
+        sb = ctx.enter_context(tc.tile_pool(name="sb", bufs=1))
+        ps = ctx.enter_context(tc.psum_pool(name="ps", bufs=1))
+
+        token_list = sb.tile([P, J // 16], U16, name="token_list")
+        a_list = sb.tile([P, M // 16], U16, name="a_list")
+        b_list = sb.tile([P, M // 16], U16, name="b_list")
+
+        x_scales = sb.tile([P, PASSES, T], U8, name="x_scales", align_bytes=64)
+        wa_planes = sb.tile([P, PASSES, N], U8, name="wa_planes", align_bytes=64)
+        nc.vector.memset(x_scales[:].rearrange("p z c -> p (z c)").bitcast(I32), 0)
+        nc.vector.memset(wa_planes[:].rearrange("p z c -> p (z c)").bitcast(I32), 0)
+
+        x_words = [sb.tile([P, T], U16, name=f"x_words{z}", align_bytes=64) for z in range(PASSES)]
+        wa_codes = [sb.tile([P, N], I32, name=f"wa_codes{z}", align_bytes=64) for z in range(PASSES)]
+        wb_raw = [sb.tile([P, PACK, N], F32, name=f"wb_raw{z}") for z in range(PASSES)]
+        bias_pairs = sb.tile([P, 2], F32, name="bias_pairs")
+        factor = sb.tile([P, HALVES], F32, name="factor")
+        x_rows = xt_scales.rearrange("z (q r) c -> r q z c", r=4)
+        wa_rows = wa_scales.rearrange("z (q r) c -> r q z c", r=4)
+        wa_src = wa_words.rearrange("z p n t -> z p (n t)")
+        wb_src = wb.rearrange("(z p t) n -> z p t n", p=P, t=PACK)
+
+        nc.sync.dma_start(token_list[:], offs)
+        for z in range(PASSES):
+            nc.sync.dma_start(x_words[z][:].bitcast(I32), xt_words[z].bitcast(I32))
+        nc.sync.dma_start(a_list[:], offs2)
+        for r in range(4):
+            nc.sync.dma_start(x_scales[r:P:32].bitcast(I32), x_rows[r].bitcast(I32))
+        nc.sync.dma_start(wb_raw[0][:], wb_src[0])
+        nc.sync.dma_start(bias_pairs[:], bi.rearrange("o (p c) -> p (o c)", c=2))
+        for r in range(4):
+            nc.sync.dma_start(wa_planes[r:P:32].bitcast(I32), wa_rows[r].bitcast(I32))
+        nc.sync.dma_start(wa_codes[0][:], wa_src[0].bitcast(I32))
+        nc.sync.dma_start(wb_raw[1][:], wb_src[1])
+        nc.sync.dma_start(wa_codes[1][:], wa_src[1].bitcast(I32))
+        nc.sync.dma_start(b_list[:], offs3)
+        with nc.allow_non_contiguous_dma(reason="one factor a partition and half"):
+            nc.sync.dma_start(factor[:], cj.rearrange("(h p) o -> p (h o)", p=P))
+
+        identity = sb.tile([P, P], F32, name="identity")
+        make_identity(nc, identity[:])
+        bias_ps = ps.tile([P, 2, P], F32, name="bias_ps")
+        for c in range(2):
+            nc.tensor.transpose(bias_ps[:, c, :], bias_pairs[:, c : c + 1].to_broadcast([P, P]), identity[:])
+        neg_factor = sb.tile([P, HALVES], F32, name="neg_factor")
+        nc.gpsimd.tensor_scalar(neg_factor[:], factor[:], -1.0, 0.0, ALU.mult, ALU.add)
+
+        picked_words = sb.tile([P, PASSES, J], U16, name="picked_words", align_bytes=64)
+        picked_scales = sb.tile([P, PASSES, J], U8, name="picked_scales", align_bytes=64)
+        for z in range(PASSES):
+            nc.vector.tensor_copy(picked_words[:, z, :], x_words[z][:].indirect(token_list[:]))
+        for z in range(PASSES):
+            nc.vector.tensor_copy(picked_scales[:, z, :], x_scales[:, z, :].indirect(token_list[:]))
+
+        def product(acc, h, z, codes, planes):
+            slots = slice(h * P, (h + 1) * P)
+            nc.tensor.matmul_mx(
+                out=acc[:],
+                lhsT=picked_words[:, z, slots].bitcast(E2M1X4),
+                lhsT_scale=picked_scales[:, z, slots],
+                rhs=codes.bitcast(E5M2X4),
+                rhs_scale=planes,
+                start=(z == 0),
+                stop=(z == PASSES - 1),
+            )
+
+        a_ps = [ps.tile([P, N], F32, name=f"a_ps{h}") for h in range(HALVES)]
+        b_ps = [ps.tile([P, N], F32, name=f"b_ps{h}") for h in range(HALVES)]
+        bias = sb.tile([P, N], F32, name="bias")
+        for z in range(PASSES):
+            grouped = sb.tile([P, N, PACK], BF16, name=f"wb_grouped{z}", align_bytes=64)
+            dst = grouped[:].rearrange("p (c i) t -> p c t i", i=4)
+            src = wb_raw[z][:].rearrange("p t (c i) -> p c t i", i=4)
+            cut = VECTOR_COLS[z] // 4
+            nc.vector.tensor_copy(dst[:, :cut], src[:, :cut])
+            nc.scalar.activation(dst[:, cut:], src[:, cut:], COPY)
+            codes = sb.tile([P, N], U32, name=f"wb_codes{z}", align_bytes=64)
+            planes = sb.tile([P, N], U8, name=f"wb_planes{z}", align_bytes=64)
+            nc.vector.quantize_mx(
+                out=codes[:].bitcast(E5M2X4), scales=planes[:], in_=grouped[:].rearrange("p n t -> p (n t)")
+            )
+            if z == 0:
+                nc.scalar.activation(
+                    bias[:].rearrange("m (p c) -> m p c", c=2), bias_ps[:].rearrange("m c p -> m p c"), COPY
+                )
+            for h in range(HALVES):
+                product(a_ps[h], h, z, wa_codes[z][:], wa_planes[:, z, :])
+            for h in range(HALVES):
+                product(b_ps[h], h, z, codes[:], planes[:])
+
+        a_picked = []
+        for h in range(HALVES):
+            a = sb.tile([P, N], F32, name=f"a{h}")
+            nc.scalar.activation(a[:], a_ps[h][:], COPY)
+            picked = sb.tile([P, M], F32, name=f"a_picked{h}")
+            nc.scalar.activation(picked[:], a[:].indirect(a_list[:]), COPY)
+            a_picked.append(picked)
+
+        b2 = []
+        for h in range(HALVES):
+            tile = sb.tile([P, N], F32, name=f"b2_{h}")
+            nc.vector.tensor_tensor(tile[:], b_ps[h][:], bias[:], ALU.add)
+            b2.append(tile)
+        for h in range(HALVES):
+            diff = sb.tile([P, M], F32, name=f"diff{h}")
+            nc.vector.tensor_tensor(diff[:], b2[h][:].indirect(b_list[:]), a_picked[h][:], ALU.subtract)
+            result = sb.tile([P, M], F32, name=f"result{h}")
+            nc.scalar.activation(result[:], diff[:], COPY, scale=neg_factor[:, h : h + 1])
+            nc.sync.dma_start(out[h * P : (h + 1) * P, :], result[:])

@@ -36,10 +36,13 @@ def tile_list_rows_onetoken_lookedtarget_kernel(
         a_list = sb.tile([P, M // 16], U16, name="a_list")
         b_list = sb.tile([P, M // 16], U16, name="b_list")
 
-        x_scales = sb.tile([P, PASSES, T], U8, name="x_scales", align_bytes=64)
+        x_scales = sb.tile([P, T], U8, name="x_scales", align_bytes=64)
+        moved_scales = sb.tile([P, J], U8, name="moved_scales", align_bytes=64)
         wa_planes = sb.tile([P, PASSES, N], U8, name="wa_planes", align_bytes=64)
-        nc.vector.memset(x_scales[:].rearrange("p z c -> p (z c)").bitcast(I32), 0)
+        nc.vector.memset(x_scales[:].bitcast(I32), 0)
         nc.vector.memset(wa_planes[:].rearrange("p z c -> p (z c)").bitcast(I32), 0)
+
+        nc.vector.memset(moved_scales[:].bitcast(I32), 0)
 
         x_words = [sb.tile([P, T], U16, name=f"x_words{z}", align_bytes=64) for z in range(PASSES)]
         wa_codes = [sb.tile([P, N], I32, name=f"wa_codes{z}", align_bytes=64) for z in range(PASSES)]
@@ -54,9 +57,10 @@ def tile_list_rows_onetoken_lookedtarget_kernel(
         nc.sync.dma_start(token_list[:], offs)
         for z in range(PASSES):
             nc.sync.dma_start(x_words[z][:].bitcast(I32), xt_words[z].bitcast(I32))
-        nc.sync.dma_start(a_list[:], offs2)
+        with nc.allow_non_contiguous_dma(reason="one factor a partition and half"):
+            nc.sync.dma_start(factor[:], cj.rearrange("(h p) o -> p (h o)", p=P))
         for r in range(4):
-            nc.sync.dma_start(x_scales[r:P:32].bitcast(I32), x_rows[r].bitcast(I32))
+            nc.sync.dma_start(x_scales[r:P:16].bitcast(I32), x_rows[r].bitcast(I32))
         nc.sync.dma_start(wb_raw[0][:], wb_src[0])
         nc.sync.dma_start(bias_pairs[:], bi.rearrange("o (p c) -> p (o c)", c=2))
         for r in range(4):
@@ -64,31 +68,32 @@ def tile_list_rows_onetoken_lookedtarget_kernel(
         nc.sync.dma_start(wa_codes[0][:], wa_src[0].bitcast(I32))
         nc.sync.dma_start(wb_raw[1][:], wb_src[1])
         nc.sync.dma_start(wa_codes[1][:], wa_src[1].bitcast(I32))
+        nc.sync.dma_start(a_list[:], offs2)
         nc.sync.dma_start(b_list[:], offs3)
-        with nc.allow_non_contiguous_dma(reason="one factor a partition and half"):
-            nc.sync.dma_start(factor[:], cj.rearrange("(h p) o -> p (h o)", p=P))
 
         identity = sb.tile([P, P], F32, name="identity")
         make_identity(nc, identity[:])
         bias_ps = ps.tile([P, 2, P], F32, name="bias_ps")
         for c in range(2):
             nc.tensor.transpose(bias_ps[:, c, :], bias_pairs[:, c : c + 1].to_broadcast([P, P]), identity[:])
-        neg_factor = sb.tile([P, HALVES], F32, name="neg_factor")
-        nc.gpsimd.tensor_scalar(neg_factor[:], factor[:], -1.0, 0.0, ALU.mult, ALU.add)
+        neg_factor = sb.tile([P, HALVES, M], F32, name="neg_factor")
+        nc.scalar.activation(neg_factor[:], factor[:].unsqueeze(2).to_broadcast([P, HALVES, M]), COPY, scale=-1.0)
 
         picked_words = sb.tile([P, PASSES, J], U16, name="picked_words", align_bytes=64)
-        picked_scales = sb.tile([P, PASSES, J], U8, name="picked_scales", align_bytes=64)
+        picked_scales = sb.tile([P, J], U8, name="picked_scales", align_bytes=64)
         for z in range(PASSES):
             nc.vector.tensor_copy(picked_words[:, z, :], x_words[z][:].indirect(token_list[:]))
-        for z in range(PASSES):
-            nc.vector.tensor_copy(picked_scales[:, z, :], x_scales[:, z, :].indirect(token_list[:]))
+        nc.vector.tensor_copy(picked_scales[:], x_scales[:].indirect(token_list[:]))
+        for r in range(4):
+            nc.sync.dma_start(moved_scales[r:P:32].bitcast(I32), picked_scales[16 + r : P : 32].bitcast(I32))
+        x_planes = [picked_scales, moved_scales]
 
         def product(acc, h, z, codes, planes):
             slots = slice(h * P, (h + 1) * P)
             nc.tensor.matmul_mx(
                 out=acc[:],
                 lhsT=picked_words[:, z, slots].bitcast(E2M1X4),
-                lhsT_scale=picked_scales[:, z, slots],
+                lhsT_scale=x_planes[z][:, slots],
                 rhs=codes.bitcast(E5M2X4),
                 rhs_scale=planes,
                 start=(z == 0),
@@ -119,22 +124,20 @@ def tile_list_rows_onetoken_lookedtarget_kernel(
             for h in range(HALVES):
                 product(b_ps[h], h, z, codes[:], planes[:])
 
-        a_picked = []
+        a = [sb.tile([P, N], F32, name=f"a{h}") for h in range(HALVES)]
+        b2 = [sb.tile([P, N], F32, name=f"b2_{h}") for h in range(HALVES)]
+        a_term = [sb.tile([P, M], F32, name=f"a_term{h}") for h in range(HALVES)]
+        b_picked = [sb.tile([P, M], F32, name=f"b_picked{h}") for h in range(HALVES)]
         for h in range(HALVES):
-            a = sb.tile([P, N], F32, name=f"a{h}")
-            nc.scalar.activation(a[:], a_ps[h][:], COPY)
-            picked = sb.tile([P, M], F32, name=f"a_picked{h}")
-            nc.scalar.activation(picked[:], a[:].indirect(a_list[:]), COPY)
-            a_picked.append(picked)
-
-        b2 = []
+            nc.scalar.activation(a[h][:], a_ps[h][:], COPY)
         for h in range(HALVES):
-            tile = sb.tile([P, N], F32, name=f"b2_{h}")
-            nc.vector.tensor_tensor(tile[:], b_ps[h][:], bias[:], ALU.add)
-            b2.append(tile)
+            nc.vector.tensor_tensor(b2[h][:], b_ps[h][:], bias[:], ALU.add)
+            nc.scalar.activation(b_picked[h][:], b2[h][:].indirect(b_list[:]), COPY)
         for h in range(HALVES):
-            diff = sb.tile([P, M], F32, name=f"diff{h}")
-            nc.vector.tensor_tensor(diff[:], b2[h][:].indirect(b_list[:]), a_picked[h][:], ALU.subtract)
+            nc.vector.tensor_tensor(a_term[h][:], a[h][:].indirect(a_list[:]), neg_factor[:, h, :], ALU.mult)
+        for h in range(HALVES):
             result = sb.tile([P, M], F32, name=f"result{h}")
-            nc.scalar.activation(result[:], diff[:], COPY, scale=neg_factor[:, h : h + 1])
+            nc.vector.scalar_tensor_tensor(
+                result[:], b_picked[h][:], neg_factor[:, h, 0:1], a_term[h][:], ALU.mult, ALU.subtract
+            )
             nc.sync.dma_start(out[h * P : (h + 1) * P, :], result[:])

@@ -36,7 +36,7 @@ def tile_list_rows_onetoken_lookedtarget_kernel(
         a_list = sb.tile([P, M // 16], U16, name="a_list")
         b_list = sb.tile([P, M // 16], U16, name="b_list")
 
-        x_scales = sb.tile([P, T], U8, name="x_scales", align_bytes=64)
+        x_scales = sb.tile([P, T], U8, name="x_scales", tag="x_scales_then_words", align_bytes=64)
         moved_scales = sb.tile([P, J], U8, name="moved_scales", align_bytes=64)
         wa_planes = sb.tile([P, PASSES, N], U8, name="wa_planes", align_bytes=64)
         nc.vector.memset(x_scales[:].bitcast(I32), 0)
@@ -45,54 +45,54 @@ def tile_list_rows_onetoken_lookedtarget_kernel(
         nc.vector.memset(moved_scales[:].bitcast(I32), 0)
 
         x_words = [sb.tile([P, T], U16, name=f"x_words{z}", align_bytes=64) for z in range(PASSES)]
-        wa_codes = [sb.tile([P, N], I32, name=f"wa_codes{z}", align_bytes=64) for z in range(PASSES)]
+        wa_codes = sb.tile([P, PASSES, N], I32, name="wa_codes", align_bytes=64)
         wb_raw = [sb.tile([P, PACK, N], F32, name=f"wb_raw{z}") for z in range(PASSES)]
         bias_pairs = sb.tile([P, 2], F32, name="bias_pairs")
         factor = sb.tile([P, HALVES], F32, name="factor")
         x_rows = xt_scales.rearrange("z (q r) c -> r q z c", r=4)
         wa_rows = wa_scales.rearrange("z (q r) c -> r q z c", r=4)
-        wa_src = wa_words.rearrange("z p n t -> z p (n t)")
         wb_src = wb.rearrange("(z p t) n -> z p t n", p=P, t=PACK)
 
         nc.sync.dma_start(token_list[:], offs)
         for z in range(PASSES):
             nc.sync.dma_start(x_words[z][:].bitcast(I32), xt_words[z].bitcast(I32))
-        with nc.allow_non_contiguous_dma(reason="one factor a partition and half"):
-            nc.sync.dma_start(factor[:], cj.rearrange("(h p) o -> p (h o)", p=P))
         for r in range(4):
             nc.sync.dma_start(x_scales[r:P:16].bitcast(I32), x_rows[r].bitcast(I32))
         nc.sync.dma_start(wb_raw[0][:], wb_src[0])
-        nc.sync.dma_start(bias_pairs[:], bi.rearrange("o (p c) -> p (o c)", c=2))
-        for r in range(4):
+        nc.sync.dma_start(wa_codes[:], wa_words.rearrange("z p n t -> p z (n t)").bitcast(I32))
+        for r in range(3):
             nc.sync.dma_start(wa_planes[r:P:32].bitcast(I32), wa_rows[r].bitcast(I32))
-        nc.sync.dma_start(wa_codes[0][:], wa_src[0].bitcast(I32))
         nc.sync.dma_start(wb_raw[1][:], wb_src[1])
-        nc.sync.dma_start(wa_codes[1][:], wa_src[1].bitcast(I32))
-        nc.sync.dma_start(a_list[:], offs2)
-        nc.sync.dma_start(b_list[:], offs3)
 
         identity = sb.tile([P, P], F32, name="identity")
         make_identity(nc, identity[:])
+        nc.gpsimd.dma_start(bias_pairs[:], bi.rearrange("o (p c) -> p (o c)", c=2))
+        for r in range(3, 4):
+            nc.gpsimd.dma_start(wa_planes[r:P:32].bitcast(I32), wa_rows[r].bitcast(I32))
+        with nc.allow_non_contiguous_dma(reason="one factor a partition and half"):
+            nc.gpsimd.dma_start(factor[:], cj.rearrange("(h p) o -> p (h o)", p=P))
         bias_ps = ps.tile([P, 2, P], F32, name="bias_ps")
         for c in range(2):
             nc.tensor.transpose(bias_ps[:, c, :], bias_pairs[:, c : c + 1].to_broadcast([P, P]), identity[:])
-        neg_factor = sb.tile([P, HALVES, M], F32, name="neg_factor")
-        nc.scalar.activation(neg_factor[:], factor[:].unsqueeze(2).to_broadcast([P, HALVES, M]), COPY, scale=-1.0)
+        neg_factor = sb.tile([P, HALVES], F32, name="neg_factor")
+        nc.gpsimd.tensor_scalar(neg_factor[:], factor[:], -1.0, 0.0, ALU.mult, ALU.add)
 
-        picked_words = sb.tile([P, PASSES, J], U16, name="picked_words", align_bytes=64)
         picked_scales = sb.tile([P, J], U8, name="picked_scales", align_bytes=64)
-        for z in range(PASSES):
-            nc.vector.tensor_copy(picked_words[:, z, :], x_words[z][:].indirect(token_list[:]))
+        picked_words = [sb.tile([P, J], U16, name="picked_words0", align_bytes=64)]
+        nc.vector.tensor_copy(picked_words[0][:], x_words[0][:].indirect(token_list[:]))
         nc.vector.tensor_copy(picked_scales[:], x_scales[:].indirect(token_list[:]))
-        for r in range(4):
-            nc.sync.dma_start(moved_scales[r:P:32].bitcast(I32), picked_scales[16 + r : P : 32].bitcast(I32))
+        nc.sync.dma_start(moved_scales[0:100].bitcast(I32), picked_scales[16:116].bitcast(I32))
+        picked_words.append(sb.tile([P, J], U16, name="picked_words1", tag="x_scales_then_words", align_bytes=64))
+        nc.vector.tensor_copy(picked_words[1][:], x_words[1][:].indirect(token_list[:]))
         x_planes = [picked_scales, moved_scales]
+        nc.sync.dma_start(a_list[:], offs2)
+        nc.sync.dma_start(b_list[:], offs3)
 
         def product(acc, h, z, codes, planes):
             slots = slice(h * P, (h + 1) * P)
             nc.tensor.matmul_mx(
                 out=acc[:],
-                lhsT=picked_words[:, z, slots].bitcast(E2M1X4),
+                lhsT=picked_words[z][:, slots].bitcast(E2M1X4),
                 lhsT_scale=x_planes[z][:, slots],
                 rhs=codes.bitcast(E5M2X4),
                 rhs_scale=planes,
@@ -120,24 +120,24 @@ def tile_list_rows_onetoken_lookedtarget_kernel(
                     bias[:].rearrange("m (p c) -> m p c", c=2), bias_ps[:].rearrange("m c p -> m p c"), COPY
                 )
             for h in range(HALVES):
-                product(a_ps[h], h, z, wa_codes[z][:], wa_planes[:, z, :])
+                product(a_ps[h], h, z, wa_codes[:, z, :], wa_planes[:, z, :])
             for h in range(HALVES):
                 product(b_ps[h], h, z, codes[:], planes[:])
 
         a = [sb.tile([P, N], F32, name=f"a{h}") for h in range(HALVES)]
         b2 = [sb.tile([P, N], F32, name=f"b2_{h}") for h in range(HALVES)]
-        a_term = [sb.tile([P, M], F32, name=f"a_term{h}") for h in range(HALVES)]
-        b_picked = [sb.tile([P, M], F32, name=f"b_picked{h}") for h in range(HALVES)]
         for h in range(HALVES):
             nc.scalar.activation(a[h][:], a_ps[h][:], COPY)
+        a_picked = [sb.tile([P, M], F32, name=f"a_picked{h}") for h in range(HALVES)]
+        for h in range(HALVES):
+            nc.scalar.activation(a_picked[h][:], a[h][:].indirect(a_list[:]), COPY)
         for h in range(HALVES):
             nc.vector.tensor_tensor(b2[h][:], b_ps[h][:], bias[:], ALU.add)
-            nc.scalar.activation(b_picked[h][:], b2[h][:].indirect(b_list[:]), COPY)
+        diff = [sb.tile([P, M], F32, name=f"diff{h}") for h in range(HALVES)]
         for h in range(HALVES):
-            nc.vector.tensor_tensor(a_term[h][:], a[h][:].indirect(a_list[:]), neg_factor[:, h, :], ALU.mult)
+            nc.vector.tensor_tensor(diff[h][:], b2[h][:].indirect(b_list[:]), a_picked[h][:], ALU.subtract)
+        result = [sb.tile([P, M], F32, name=f"result{h}") for h in range(HALVES)]
+        nc.scalar.activation(result[0][:], diff[0][:], COPY, scale=neg_factor[:, 0:1])
+        nc.vector.tensor_scalar(result[1][:], diff[1][:], neg_factor[:, 1:2], None, ALU.mult)
         for h in range(HALVES):
-            result = sb.tile([P, M], F32, name=f"result{h}")
-            nc.vector.scalar_tensor_tensor(
-                result[:], b_picked[h][:], neg_factor[:, h, 0:1], a_term[h][:], ALU.mult, ALU.subtract
-            )
-            nc.sync.dma_start(out[h * P : (h + 1) * P, :], result[:])
+            nc.sync.dma_start(out[h * P : (h + 1) * P, :], result[h][:])

from contextlib import ExitStack

import concourse.mybir as mybir
from concourse.masks import make_identity

K, T, J, N, M = 1024, 1024, 256, 256, 128
FLOPS = 2 * 2 * K * J * N

F32 = mybir.dt.float32
BF16 = mybir.dt.bfloat16
I32 = mybir.dt.int32
U32 = mybir.dt.uint32
U16 = mybir.dt.uint16
U8 = mybir.dt.uint8
E5M2X4 = mybir.dt.float8_e5m2_x4
E2M1X4 = mybir.dt.float4_e2m1fn_x4
ALU = mybir.AluOpType
COPY = mybir.ActivationFunctionType.Copy

P = 128
PACK = 4
PASSES = K // (P * PACK)
HALVES = J // P
VECTOR_COLS = (128, 168)


def tile_list_rows_onetoken_lookedtarget_kernel(
    tc, xt_words, xt_scales, wa_words, wa_scales, wb, bi, cj, offs, offs2, offs3, out
):
    nc = tc.nc
    with ExitStack() as ctx:
        sb = ctx.enter_context(tc.tile_pool(name="sb", bufs=1))
        ps = ctx.enter_context(tc.psum_pool(name="ps", bufs=1))

        token_list = sb.tile([P, J // 16], U16, name="token_list")
        a_list = sb.tile([P, M // 16], U16, name="a_list")
        b_list = sb.tile([P, M // 16], U16, name="b_list")

        x_scales = sb.tile([P, T], U8, name="x_scales", tag="x_scales_then_words", align_bytes=64)
        moved_scales = sb.tile([P, J], U8, name="moved_scales", align_bytes=64)
        wa_planes = sb.tile([P, PASSES, N], U8, name="wa_planes", align_bytes=64)
        nc.vector.memset(x_scales[:].bitcast(I32), 0)
        nc.vector.memset(wa_planes[:].rearrange("p z c -> p (z c)").bitcast(I32), 0)

        nc.vector.memset(moved_scales[:].bitcast(I32), 0)

        x_words = [sb.tile([P, T], U16, name=f"x_words{z}", align_bytes=64) for z in range(PASSES)]
        wa_codes = sb.tile([P, PASSES, N], I32, name="wa_codes", align_bytes=64)
        wb_raw = [sb.tile([P, PACK, N], F32, name=f"wb_raw{z}") for z in range(PASSES)]
        bias_pairs = sb.tile([P, 2], F32, name="bias_pairs")
        factor = sb.tile([P, HALVES], F32, name="factor")
        x_rows = xt_scales.rearrange("z (q r) c -> r q z c", r=4)
        wa_rows = wa_scales.rearrange("z (q r) c -> r q z c", r=4)
        wb_src = wb.rearrange("(z p t) n -> z p t n", p=P, t=PACK)

        nc.sync.dma_start(token_list[:], offs)
        for z in range(PASSES):
            nc.sync.dma_start(x_words[z][:].bitcast(I32), xt_words[z].bitcast(I32))
        for r in range(4):
            nc.sync.dma_start(x_scales[r:P:16].bitcast(I32), x_rows[r].bitcast(I32))
        nc.sync.dma_start(wb_raw[0][:], wb_src[0])
        nc.sync.dma_start(wa_codes[:], wa_words.rearrange("z p n t -> p z (n t)").bitcast(I32))
        for r in range(3):
            nc.sync.dma_start(wa_planes[r:P:32].bitcast(I32), wa_rows[r].bitcast(I32))
        nc.sync.dma_start(wb_raw[1][:], wb_src[1])

        identity = sb.tile([P, P], F32, name="identity")
        make_identity(nc, identity[:])
        nc.gpsimd.dma_start(bias_pairs[:], bi.rearrange("o (p c) -> p (o c)", c=2))
        for r in range(3, 4):
            nc.gpsimd.dma_start(wa_planes[r:P:32].bitcast(I32), wa_rows[r].bitcast(I32))
        with nc.allow_non_contiguous_dma(reason="one factor a partition and half"):
            nc.gpsimd.dma_start(factor[:], cj.rearrange("(h p) o -> p (h o)", p=P))
        bias_ps = ps.tile([P, 2, P], F32, name="bias_ps")
        for c in range(2):
            nc.tensor.transpose(bias_ps[:, c, :], bias_pairs[:, c : c + 1].to_broadcast([P, P]), identity[:])
        neg_factor = sb.tile([P, HALVES], F32, name="neg_factor")
        nc.gpsimd.tensor_scalar(neg_factor[:], factor[:], -1.0, 0.0, ALU.mult, ALU.add)

        picked_scales = sb.tile([P, J], U8, name="picked_scales", align_bytes=64)
        picked_words = [sb.tile([P, J], U16, name="picked_words0", align_bytes=64)]
        nc.vector.tensor_copy(picked_words[0][:], x_words[0][:].indirect(token_list[:]))
        nc.vector.tensor_copy(picked_scales[:], x_scales[:].indirect(token_list[:]))
        nc.sync.dma_start(moved_scales[0:100].bitcast(I32), picked_scales[16:116].bitcast(I32))
        picked_words.append(sb.tile([P, J], U16, name="picked_words1", tag="x_scales_then_words", align_bytes=64))
        nc.vector.tensor_copy(picked_words[1][:], x_words[1][:].indirect(token_list[:]))
        x_planes = [picked_scales, moved_scales]
        nc.sync.dma_start(a_list[:], offs2)
        nc.sync.dma_start(b_list[:], offs3)

        def product(acc, h, z, codes, planes):
            slots = slice(h * P, (h + 1) * P)
            nc.tensor.matmul_mx(
                out=acc[:],
                lhsT=picked_words[z][:, slots].bitcast(E2M1X4),
                lhsT_scale=x_planes[z][:, slots],
                rhs=codes.bitcast(E5M2X4),
                rhs_scale=planes,
                start=(z == 0),
                stop=(z == PASSES - 1),
            )

        a_ps = [ps.tile([P, N], F32, name=f"a_ps{h}") for h in range(HALVES)]
        b_ps = [ps.tile([P, N], F32, name=f"b_ps{h}") for h in range(HALVES)]
        bias = sb.tile([P, N], F32, name="bias")
        for z in range(PASSES):
            grouped = sb.tile([P, N, PACK], BF16, name=f"wb_grouped{z}", align_bytes=64)
            dst = grouped[:].rearrange("p (c i) t -> p c t i", i=4)
            src = wb_raw[z][:].rearrange("p t (c i) -> p c t i", i=4)
            cut = VECTOR_COLS[z] // 4
            nc.vector.tensor_copy(dst[:, :cut], src[:, :cut])
            nc.scalar.activation(dst[:, cut:], src[:, cut:], COPY)
            codes = sb.tile([P, N], U32, name=f"wb_codes{z}", align_bytes=64)
            planes = sb.tile([P, N], U8, name=f"wb_planes{z}", align_bytes=64)
            nc.vector.quantize_mx(
                out=codes[:].bitcast(E5M2X4), scales=planes[:], in_=grouped[:].rearrange("p n t -> p (n t)")
            )
            if z == 0:
                nc.scalar.activation(
                    bias[:].rearrange("m (p c) -> m p c", c=2), bias_ps[:].rearrange("m c p -> m p c"), COPY
                )
            for h in range(HALVES):
                product(a_ps[h], h, z, wa_codes[:, z, :], wa_planes[:, z, :])
            for h in range(HALVES):
                product(b_ps[h], h, z, codes[:], planes[:])

        a = [sb.tile([P, N], F32, name=f"a{h}") for h in range(HALVES)]
        b2 = [sb.tile([P, N], F32, name=f"b2_{h}") for h in range(HALVES)]
        for h in range(HALVES):
            nc.scalar.activation(a[h][:], a_ps[h][:], COPY)
        a_picked = [sb.tile([P, M], F32, name=f"a_picked{h}") for h in range(HALVES)]
        for h in range(HALVES):
            nc.scalar.activation(a_picked[h][:], a[h][:].indirect(a_list[:]), COPY)
        for h in range(HALVES):
            nc.vector.tensor_tensor(b2[h][:], b_ps[h][:], bias[:], ALU.add)
        diff = [sb.tile([P, M], F32, name=f"diff{h}") for h in range(HALVES)]
        for h in range(HALVES):
            nc.vector.tensor_tensor(diff[h][:], b2[h][:].indirect(b_list[:]), a_picked[h][:], ALU.subtract)
        result = [sb.tile([P, M], F32, name=f"result{h}") for h in range(HALVES)]
        nc.scalar.activation(result[0][:], diff[0][:], COPY, scale=neg_factor[:, 0:1])
        nc.vector.tensor_scalar(result[1][:], diff[1][:], neg_factor[:, 1:2], None, ALU.mult)
        for h in range(HALVES):
            nc.sync.dma_start(out[h * P : (h + 1) * P, :], result[h][:])
